import numpy as np, ml_dtypes
CORES = [8,11,14,16,19,22,24,27,30]
N = 9
import mx_ref
NC, G = 128, 2
C = np.float32(0.047)
CNT = [[0,0,60,4,0,0,0,48,16],[36,0,4,32,0,12,0,16,28],[4,16,0,32,28,4,28,16,0],[0,24,0,0,20,52,12,4,16],[40,4,16,24,0,0,24,0,20],[20,28,20,0,16,0,0,28,16],[28,16,12,0,24,32,0,0,16],[0,40,0,0,28,4,40,0,16],[0,0,16,36,12,24,24,16,0]]
OFF = [[sum(c[:e]) for e in range(N + 1)] for c in CNT]
BF = ml_dtypes.bfloat16
def cut(t, i, w=512):
    return t[:, w * i:w * i + w]
def tile(rs):
    return np.stack(rs, axis=2).reshape(128, -1).astype(BF)
def layer(w, X):
    out = []
    for i in range(G):
        for t in range(len(X)):
            p = mx_ref.matmul(mx_ref.quantize(cut(w, len(X) * i + t)), X[t])
            z = p if t == 0 else z + p
        out.append(z)
    return out
def act(Z):
    return [np.maximum(s * z, 0) * C for z in Z for s in (1, -1)]
def setup_inputs(rng):
    def f(*shape):
        return mx_ref.flush((rng.standard_normal(shape, dtype=np.float32) * np.exp2(rng.integers(-2, 3, shape[:-1] + (1,)))).astype(BF))
    return {"x": f(N, 128, 4 * NC), "w1": f(N, 128, G * 512), "w2": f(N, 128, 512)}
def setup_inputs_blocks(rng):
    d = setup_inputs(rng)
    for k in ("x", "w1", "w2"): d[k] = mx_ref.spread(d[k], rng, 4)
    return d
def setup_inputs_wide(rng):
    d = setup_inputs(rng)
    for k in ("x", "w1", "w2"): d[k] = mx_ref.flush((d[k].astype(np.float32) * np.exp2(rng.integers(-8, 9, (N, 1, 1))).astype(np.float32)).astype(BF))
    return d
def setup_inputs_zeros(rng):
    d = setup_inputs(rng); v = d["x"].reshape(N, 128, -1, 4).copy()
    v[np.broadcast_to((rng.random((N, 1, v.shape[2], 1)) < 0.33), v.shape)] = 0
    d["x"] = v.reshape(d["x"].shape)
    return d
def reference(x, w1, w2):
    y = np.zeros((N, 128, NC), np.float32)
    for e in range(N):
        t = np.concatenate([x[j][:, 4 * OFF[j][e]:4 * OFF[j][e + 1]] for j in range(N)], axis=1)
        p = mx_ref.matmul(mx_ref.quantize(w2[e]), mx_ref.quantize(tile(act(layer(w1[e], [mx_ref.quantize(t)])))))
        y[e] = p
    return {"y": y}

import math
from concourse.bass import DstId, RemoteDMATransfer
from concourse.mybir import dt, AluOpType, ActivationFunctionType

NT = 128
LZ = 32
GAP = 32
NATW = LZ + NT + 32
NREG = 3
XQW = NATW + NREG * (GAP + NT)
ML = 64
BW = ML + 512 + 64
LAM = 16
CACT = 0.047

SCRATCH = {
    "xt": ("sbuf", [128, 4 * (LZ + 2 * NT)], "bfloat16"),
    "w1t": ("sbuf", [128, 1024], "bfloat16"),
    "w2t": ("sbuf", [128, 512], "bfloat16"),
    "xq": ("sbuf", [128, XQW], "float8_e4m3fn_x4"),
    "xs": ("sbuf", [128, XQW], "uint8"),
    "w1q": ("sbuf", [128, 256], "float8_e4m3fn_x4"),
    "w1s": ("sbuf", [128, 256], "uint8"),
    "w2q": ("sbuf", [128, 128], "float8_e4m3fn_x4"),
    "w2s": ("sbuf", [128, 128], "uint8"),
    "bq": ("sbuf", [128, BW], "float8_e4m3fn_x4"),
    "bs": ("sbuf", [128, BW], "uint8"),
    "h": ("sbuf", [128, 2048], "bfloat16"),
    "hq": ("sbuf", [128, 512], "float8_e4m3fn_x4"),
    "hs": ("sbuf", [128, 512], "uint8"),
    "ysb": ("sbuf", [128, 128], "float32"),
    "z": ("psum", [128, 1024], "float32"),
    "p": ("psum", [128, 512], "float32"),
}
SEMAPHORES = ["ldx", "ldm", "ldr", "ldw1", "ldw2", "qx", "qr", "qw1", "qw2", "arr", "leg", "sent",
              "z0", "z1", "act", "hqd", "pd", "cp", "st"]


def _bits(mask):
    return [b for b in range(16) if (mask >> b) & 1]


def _classes(items, lam):
    n = len(items)
    best = [(0.0, [])] + [None] * n
    for hi in range(1, n + 1):
        for lo in range(hi):
            w = items[lo]["v"]
            c = lam
            kinds = [it["kind"] for it in items[lo:hi] if it["on"]]
            if "leg" in kinds and "dir" in kinds:
                c = math.inf
            for it in items[lo:hi]:
                pad = w - it["v"]
                if pad > it["avail"]:
                    c = math.inf
                elif not it["free"]:
                    c += pad + (2 if pad else 0)
            if best[lo] is not None and c < math.inf:
                t = best[lo][0] + c
                if best[hi] is None or t < best[hi][0]:
                    best[hi] = (t, best[lo][1] + [(lo, hi)])
    for lo, hi in best[n][1]:
        for it in items[lo:hi]:
            it["w"] = items[lo]["v"]


def make_plan(cores, CNT, topo, lam=LAM):
    N = len(cores)
    OFF = [[sum(r[:e]) for e in range(N + 1)] for r in CNT]
    sends = [[] for _ in range(N)]
    pieces = [[] for _ in range(N)]
    regions = [[] for _ in range(N)]
    for e in range(N):
        if CNT[e][e]:
            raise ValueError("own columns are not handled")
        pend = None
        for j in range(N):
            c = CNT[j][e]
            if not c:
                continue
            if not topo.may_write(cores[j], cores[e]):
                if pend is not None:
                    raise ValueError("two legs in a row")
                pend = j
                continue
            it = {"kind": "dir", "e": e, "s": j, "v": c, "src": LZ + OFF[j][e], "dst": cores[e], "own": c}
            if pend is not None:
                i = pend
                pend = None
                if topo.chip(cores[i]) != topo.chip(cores[j]):
                    raise ValueError("no relay on the chip")
                rs = NATW + len(regions[j]) * (GAP + NT) + GAP
                regions[j].append((OFF[j][e], rs))
                lc = CNT[i][e]
                sends[i].append({"kind": "leg", "e": e, "s": i, "v": lc, "src": LZ + OFF[i][e], "dst": cores[j],
                                 "end": rs, "free": True, "side": "L", "avail": min(GAP - lc, LZ + OFF[i][e])})
                it.update(kind="mrg", v=c + lc, src=rs - lc)
            pieces[e].append(it)
            sends[j].append(it)
        if pend is not None:
            raise ValueError("leg without a relay")
    for e in range(N):
        for k, it in enumerate(pieces[e]):
            if k == len(pieces[e]) - 1:
                it.update(side="R", free=True)
            elif k == 0 and it["kind"] == "dir":
                it.update(side="L", free=True)
            else:
                it.update(side="R", free=False)
            if it["kind"] == "mrg":
                it["avail"] = NT - it["own"]
            elif it["side"] == "L":
                it["avail"] = min(it["src"], ML)
            else:
                it["avail"] = NATW - (it["src"] + it["v"])
    for s in range(N):
        for it in sends[s]:
            it["on"] = topo.chip(it["dst"]) == topo.chip(cores[s])
        for stage in (("leg", "dir"), ("mrg",)):
            its = sorted([it for it in sends[s] if it["kind"] in stage], key=lambda t: -t["v"])
            if its:
                _classes(its, lam)
    recv = []
    for e in range(N):
        cur = None
        segs = []
        ycol = 0
        for it in pieces[e]:
            pad = it["w"] - it["v"]
            pl = pad if it["side"] == "L" else 0
            if cur is None:
                cur = ML - pl
            it["d0"] = cur
            it["s0"] = it["src"] - pl
            v0 = cur + pl
            if segs and segs[-1][0] + segs[-1][1] == v0:
                segs[-1][1] += it["v"]
            else:
                segs.append([v0, it["v"], ycol])
            ycol += it["v"]
            cur += it["w"]
        if cur > BW or ycol != NT:
            raise ValueError("landing buffer")
        recv.append({"v0": ML, "n": segs[-1][0] + segs[-1][1] - ML, "segs": segs, "arr": 0})
    plan = []
    legsum = [0] * N
    for s in range(N):
        me = cores[s]
        offc = [it for it in sends[s] if not it["on"]]
        offpool = _bits(topo.mask(me, offc[0]["dst"])) if offc else []
        onc = [it for it in sends[s] if it["on"]]
        onpool = [b for b in _bits(topo.mask(me, onc[0]["dst"])) if b not in offpool] if onc else []
        load = [0.0] * 16
        lo, hi = LZ, LZ + NT
        stages = []
        for stage in (("leg", "dir"), ("mrg",)):
            bywidth = {}
            for it in sends[s]:
                if it["kind"] not in stage:
                    continue
                if it["kind"] == "leg":
                    it["s0"] = it["src"] - (it["w"] - it["v"])
                    it["d0"] = it["end"] - it["w"]
                if it["kind"] != "mrg":
                    lo, hi = min(lo, it["s0"]), max(hi, it["s0"] + it["w"])
                for plane in (0, 1):
                    bywidth.setdefault(it["w"] * (1 if plane else 4), []).append((it, plane))
            calls = []
            for nbytes, trs in bywidth.items():
                call = []
                for pool, part in ((offpool, [t for t in trs if not t[0]["on"]]),
                                   (onpool, [t for t in trs if t[0]["on"]])):
                    if not part:
                        continue
                    if len(part) > len(pool):
                        raise ValueError("too many transfers for a call")
                    size = [1] * len(part)
                    while True:
                        k = min(range(len(part)), key=lambda q: size[q])
                        if sum(size) + size[k] > len(pool):
                            break
                        size[k] *= 2
                    free = sorted(pool, key=lambda b: load[b])
                    for k in sorted(range(len(part)), key=lambda q: size[q]):
                        eng, free = free[:size[k]], free[size[k]:]
                        for b in eng:
                            load[b] += (128 // size[k]) * (1.0 + nbytes / 512.0)
                        call.append({"it": part[k][0], "plane": part[k][1], "eng": eng, "bytes": nbytes})
                calls.append(call)
            calls.sort(key=lambda c: (0 if any(t["it"]["kind"] == "leg" for t in c) else 1, -c[0]["bytes"]))
            stages.append(calls)
        sent = 0
        for calls in stages:
            for call in calls:
                for t in call:
                    k = len(t["eng"])
                    sent += k
                    if t["it"]["kind"] == "leg":
                        legsum[cores.index(t["it"]["dst"])] += k
                    else:
                        recv[t["it"]["e"]]["arr"] += k
        plan.append({"stages": stages, "sent": sent, "view": (lo, hi + (hi - lo) % 2), "regions": regions[s],
                     "load": load})
    for s in range(N):
        plan[s]["recv"] = recv[s]
        plan[s]["legs"] = legsum[s]
    return plan


def rank_program(g, core, T, topo):
    rank = T.rank_of(core)
    if rank is None:
        return
    P = make_plan(list(T.cores), T.tables["CNT"], topo)[rank]
    S = T.sem
    sy, sc, ve, te = g.sync, g.scalar, g.vector, g.tensor
    u8 = dt.uint8

    lo, hi = P["view"]
    xe = LZ + NT
    right = max([hi] + [LZ + a + NT for a, _ in P["regions"]])
    sy.dma_start(T.xt[:, 4 * LZ:4 * xe], T.x[:, :]).then_inc(S.ldx, 16)
    nm = 0
    if lo < LZ:
        sc.dma_start(T.xt[:, 4 * lo:4 * LZ], T.x[:, 4 * (NT - LZ + lo):4 * NT]).then_inc(S.ldm, 16)
        nm += 16
    if hi > xe:
        sc.dma_start(T.xt[:, 4 * xe:4 * hi], T.x[:, 0:4 * (hi - xe)]).then_inc(S.ldm, 16)
        nm += 16
    if right > hi:
        sc.dma_start(T.xt[:, 4 * hi:4 * right], T.x[:, 4 * (hi - xe):4 * (right - xe)]).then_inc(S.ldr, 16)
    sy.dma_start(T.w1t[:, :], T.w1[:, :]).then_inc(S.ldw1, 16)
    sy.dma_start(T.w2t[:, :], T.w2[:, :]).then_inc(S.ldw2, 16)

    ve.wait_ge(S.ldx, 16)
    if nm:
        ve.wait_ge(S.ldm, nm)
    ve.quantize_mx(T.xq[:, lo:hi], T.xs[:, lo:hi], T.xt[:, 4 * lo:4 * hi]).then_inc(S.qx, 1)
    if right > hi:
        ve.wait_ge(S.ldr, 16)
    for a, rs in P["regions"]:
        ve.quantize_mx(T.xq[:, rs:rs + NT], T.xs[:, rs:rs + NT],
                       T.xt[:, 4 * (LZ + a):4 * (LZ + a + NT)]).then_inc(S.qr, 1)
    ve.wait_ge(S.ldw1, 16)
    ve.quantize_mx(T.w1q[:, :], T.w1s[:, :], T.w1t[:, :]).then_inc(S.qw1, 1)
    ve.wait_ge(S.ldw2, 16)
    ve.quantize_mx(T.w2q[:, :], T.w2s[:, :], T.w2t[:, :]).then_inc(S.qw2, 1)

    g.wait_ge(S.qx, 1)
    for k, calls in enumerate(P["stages"]):
        if k == 1 and calls:
            g.wait_ge(S.qr, len(P["regions"]))
            g.wait_ge(S.leg, P["legs"])
        for call in calls:
            trs = []
            for t in call:
                it = t["it"]
                w, s0, d0 = it["w"], it["s0"], it["d0"]
                leg = it["kind"] == "leg"
                if t["plane"]:
                    src = T.xs[:, s0:s0 + w]
                    dst = (T.xs if leg else T.bs)[:, d0:d0 + w]
                else:
                    src = T.xq[:, s0:s0 + w].bitcast(u8)
                    dst = (T.xq if leg else T.bq)[:, d0:d0 + w].bitcast(u8)
                rid, pid, _ = topo.addr(it["dst"])
                trs.append(RemoteDMATransfer(dst_ids=[DstId(rid=rid, pnc=pid)],
                                             dma_engine_mask=sum(1 << b for b in t["eng"]),
                                             remote_sem=S.leg if leg else S.arr, src=src, dst=dst))
            g.remote_dma_fused(trs, local_sem=S.sent)

    R = P["recv"]
    v0, n = R["v0"], R["n"]
    te.wait_ge(S.qw1, 1)
    te.wait_ge(S.arr, R["arr"])
    te.matmul_mx(T.z[:, 0:n], T.w1q[:, 0:128], T.w1s[:, 0:128], T.bq[:, v0:v0 + n], T.bs[:, v0:v0 + n],
                 True, True).then_inc(S.z0, 1)
    te.matmul_mx(T.z[:, 512:512 + n], T.w1q[:, 128:256], T.w1s[:, 128:256], T.bq[:, v0:v0 + n], T.bs[:, v0:v0 + n],
                 True, True).then_inc(S.z1, 1)
    ve.wait_ge(S.z0, 1)
    ve.tensor_scalar(T.h[:, 0:4 * n:4], T.z[:, 0:n], 0.0, CACT, AluOpType.max, AluOpType.mult).then_inc(S.act, 1)
    ve.tensor_scalar(T.h[:, 1:4 * n:4], T.z[:, 0:n], -CACT, 0.0, AluOpType.mult, AluOpType.max).then_inc(S.act, 1)
    sc.wait_ge(S.z1, 1)
    sc.activation(T.h[:, 2:4 * n:4], T.z[:, 512:512 + n], ActivationFunctionType.Relu, scale=CACT).then_inc(S.act, 1)
    sc.activation(T.h[:, 3:4 * n:4], T.z[:, 512:512 + n], ActivationFunctionType.Relu, scale=-CACT).then_inc(S.act, 1)
    ve.wait_ge(S.act, 4)
    ve.quantize_mx(T.hq[:, 0:n], T.hs[:, 0:n], T.h[:, 0:4 * n]).then_inc(S.hqd, 1)
    te.wait_ge(S.qw2, 1)
    te.wait_ge(S.hqd, 1)
    te.matmul_mx(T.p[:, 0:n], T.w2q[:, :], T.w2s[:, :], T.hq[:, 0:n], T.hs[:, 0:n], True, True).then_inc(S.pd, 1)
    ve.wait_ge(S.pd, 1)
    for b0, ln, y0 in R["segs"]:
        ve.tensor_copy(T.ysb[:, y0:y0 + ln], T.p[:, b0 - v0:b0 - v0 + ln]).then_inc(S.cp, 1)
    sy.wait_ge(S.cp, len(R["segs"]))
    sy.dma_start(T.y[:, :], T.ysb[:, :]).then_inc(S.st, 16)
    sy.wait_ge(S.st, 16)
    g.wait_ge(S.sent, P["sent"])
